import numpy as np, ml_dtypes
CORES = [0,1,2,3]
N = 4
ROOT = 3
WIDTHS = [3,40,1,24]
XW = 40
def setup_inputs(rng):
    return {"x": rng.standard_normal((N, 128, XW), dtype=np.float32).astype(ml_dtypes.bfloat16)}
def reference(x):
    g = np.concatenate([x[r][:, :WIDTHS[r]] for r in range(N)], axis=1)
    y = np.full((N, 128, g.shape[1]), np.nan, x.dtype)
    y[ROOT] = g
    return {"y": y}

SCRATCH = {
    "stage": ("sbuf", [128, 40], "bfloat16"),
    "land": ("sbuf", [128, 68], "bfloat16"),
}
SEMAPHORES = ["loaded", "read", "arrived", "stored"]

ENGINES = 16


def rank_program(g, core, T, topo):
    rank = T.rank_of(core)
    if rank is None:
        return

    widths = T.tables["WIDTHS"]
    n = len(widths)
    root = n - 1 if T.root is None else T.root
    off = [sum(widths[:r]) for r in range(n)]
    w = widths[rank]

    if rank == root:
        g.sync.dma_start(T.land[:, off[rank]:off[rank] + w], T.x[:, 0:w]).then_inc(T.sem.arrived, 16)
        g.sync.wait_ge(T.sem.arrived, ENGINES * (n - 1) + 16)
        g.sync.dma_start(T.y[:, :], T.land[:, :]).then_inc(T.sem.stored, 16)
        g.sync.wait_ge(T.sem.stored, 16)
        return

    lw = max(w, 2)
    g.sync.dma_start(T.stage[:, 0:lw], T.x[:, 0:lw]).then_inc(T.sem.loaded, 16)
    g.wait_ge(T.sem.loaded, 16)
    dst = T.cores[root]
    rid, pid, _se = topo.addr(dst)
    g.remote_dma(
        T.land[:, off[rank]:off[rank] + w],
        T.stage[:, 0:w],
        remote_sem=T.sem.arrived,
        local_sem=T.sem.read,
        pid=pid,
        routing_id=rid,
        dma_engine_mask=topo.mask(core, dst),
    )
    g.wait_ge(T.sem.read, ENGINES)
